import numpy as np
import ml_dtypes


def mxq(x, axis, fmt="e4m3"):
    dtype, down = {"e4m3": (ml_dtypes.float8_e4m3fn, 7), "e5m2": (ml_dtypes.float8_e5m2, 14)}[fmt]
    v = np.moveaxis(np.asarray(x, np.float32).astype(ml_dtypes.bfloat16).astype(np.float64), axis, -1)
    blocks = v.reshape(v.shape[:-1] + (-1, 32))
    amax = np.abs(blocks).max(-1, keepdims=True)
    byte = np.maximum(np.where(amax > 0, np.frexp(amax)[1] - 1 + 127, 0) - down, 1)
    scale = np.exp2(byte - 127.0)
    codes = (blocks / scale).astype(np.float32).astype(dtype).astype(np.float64)
    return np.moveaxis((codes * scale).reshape(v.shape), -1, axis)


WIDE = False


def mx_kscale(k):
    if not WIDE:
        return np.ones(k)
    levels = np.array([10, -10, 5, -5, 0])
    if k % 512:
        return np.exp2(np.random.permutation(np.resize(levels, k // 32))).repeat(32)
    a = np.empty((k // 512, 16))
    for p in range(k // 512):
        a[p, :8] = np.random.permutation(np.resize(levels, 8))
        for g in range(8):
            far = levels[np.abs(levels - a[p, g]) >= 10]
            a[p, g + 8] = far[np.random.randint(len(far))]
    return np.exp2(a.ravel()).repeat(32)


def f64(x):
    return np.asarray(x).astype(np.float64)


def striped(idx):
    return np.tile(idx.reshape(-1, 16).T, (8, 1)).astype(np.uint16)


def unstriped(offs):
    return offs[:16].T.reshape(-1).astype(np.int64)


def striped8(idx):
    return np.concatenate([x.reshape(-1, 16).T for x in idx]).astype(np.uint16)


def runs(offs, k):
    lists = np.stack([offs[16 * r : 16 * r + 16].T.reshape(-1) for r in range(8)]).astype(np.int64)
    return lists[np.arange(k) % 512 // 64]


def pack_weight(w):
    k, n = w.shape
    w = f64(np.asarray(w, np.float32).astype(ml_dtypes.bfloat16)).reshape(k // 32, 32, n)
    amax = np.abs(w).max(1)
    byte = np.clip(np.where(amax > 0, np.frexp(amax)[1] - 1 + 127 - 7, 1), 1, 254)
    scaled = (w * np.exp2(127.0 - byte)[:, None, :]).reshape(k, n).astype(np.float32)
    words = np.ascontiguousarray(scaled.reshape(k // 512, 128, 4, n).transpose(0, 1, 3, 2)).astype(ml_dtypes.float8_e4m3fn).view(np.uint8)
    return words, np.ascontiguousarray(byte.astype(np.uint8).reshape(k // 512, 16, n))


def unpack_weight(words, scales):
    g, p, n, _ = words.shape
    vals = np.ascontiguousarray(words).view(ml_dtypes.float8_e4m3fn).astype(np.float64) * np.repeat(np.exp2(scales.astype(np.float64) - 127.0), 8, axis=1)[..., None]
    return vals.transpose(0, 1, 3, 2).reshape(g * 512, n)


K, T, S, N, H = 512, 2048, 512, 512, 512


def setup_inputs():
    n = np.random.standard_normal
    s = mx_kscale(K)[:, None]
    u = mx_kscale(H)
    packed_xT = pack_weight(n((K, T)) * s)
    return {
        "x_words": packed_xT[0],
        "x_scales": packed_xT[1],
        "w1": (n((K, H)) / np.sqrt(K) / s).astype(np.float32),
        "gn": (np.random.uniform(0.5, 1.5, (H, 1)) * u[:, None]).astype(np.float32),
        "w2": (n((H, N)) / np.sqrt(H) / u[:, None]).astype(np.float32),
        "w3": (n((K, N)) / np.sqrt(K) / s).astype(np.float32),
        "offs": striped(np.random.permutation(T)[:S]),
        "n1": striped8(np.stack([np.random.permutation(S) for _ in range(8)])),
        "n2": striped8(np.stack([np.random.permutation(S) for _ in range(8)])),
        "two": striped(np.random.permutation(T)[:S]),
        "n3": striped8(np.stack([np.random.permutation(S) for _ in range(8)])),
        "n4": striped8(np.stack([np.random.permutation(S) for _ in range(8)])),
    }


def reference(x_words, x_scales, w1, gn, w2, w3, offs, n1, n2, two, n3, n4):
    xq = unpack_weight(x_words, x_scales)[:, unstriped(offs)]
    y = mxq(f64(w1), 0, "e4m3").T @ xq
    sq = (y) ** 2
    z = f64(gn) * ((y[np.arange(H)[:, None], runs(n2, H)]) / (np.sqrt(sq + sq[np.arange(H)[:, None], runs(n1, H)] + 0.25)))
    h = mxq(f64(w2), 0, "e4m3").T @ mxq(z, 0, "e4m3")
    x_two = unpack_weight(x_words, x_scales)[:, unstriped(two)]
    d = mxq(f64(w3), 0, "e4m3").T @ x_two
    return np.maximum(h, d[np.arange(N)[:, None], runs(n4, N)]) - (np.minimum(h[np.arange(N)[:, None], runs(n3, N)], d))

@@ -1,0 +1,190 @@
+from contextlib import ExitStack
+
+import concourse.mybir as mybir
+from concourse.masks import make_identity
+
+K, T, S, N, H = 512, 2048, 512, 512, 512
+FLOPS = 3 * 2 * 512 * 512 * 512
+
+F32 = mybir.dt.float32
+BF16 = mybir.dt.bfloat16
+I32 = mybir.dt.int32
+U32 = mybir.dt.uint32
+U16 = mybir.dt.uint16
+U8 = mybir.dt.uint8
+FP8X4 = mybir.dt.float8_e4m3fn_x4
+ALU = mybir.AluOpType
+ACT = mybir.ActivationFunctionType
+
+P = 128
+PACK = 4
+WINDOW = 2 * S
+
+
+def tile_picked_latemaxbrms_none_p_kernel(tc, x_words, x_scales, w1, gn, w2, w3, offs, n1, n2, two, n3, n4, out):
+    nc = tc.nc
+    with ExitStack() as ctx:
+        keep = ctx.enter_context(tc.tile_pool(name="keep", bufs=1))
+        psum = ctx.enter_context(tc.psum_pool(name="psum", bufs=1))
+
+        def load_list(name, src):
+            lst = keep.tile([P, S // 16], U16, name=name)
+            nc.sync.dma_start(lst[:], src)
+            return lst
+
+        def load_weight_half(name, w, half):
+            raw = keep.tile([P, PACK, N // 2], F32, name=name)
+            cols = slice(half * N // 2, (half + 1) * N // 2)
+            nc.sync.dma_start(out=raw[:], in_=w[:, cols].rearrange("(p j) c -> p j c", j=PACK))
+            return raw
+
+        def weave_views(grouped, raw, half, m0, m1):
+            dst = grouped[:].rearrange("p (t m j) -> p m j t", t=PACK, j=PACK)[:, half * P // 2 + m0 : half * P // 2 + m1]
+            return dst, raw[:].rearrange("p j (m t) -> p m j t", t=PACK)[:, m0:m1]
+
+        def quantize(codes, scales, grouped, c0, c1):
+            nc.vector.quantize_mx(out=codes[:, c0:c1].bitcast(FP8X4), scales=scales[:, c0:c1], in_=grouped[:, PACK * c0 : PACK * c1])
+
+        def product(bank, wq, ws, t, xq, xs, c0, c1):
+            cols = slice(t * P, (t + 1) * P)
+            nc.tensor.matmul_mx(out=bank[:, c0:c1], lhsT=wq[:, cols].bitcast(FP8X4), lhsT_scale=ws[:, cols],
+                                rhs=xq[:, c0:c1].bitcast(FP8X4), rhs_scale=xs[:, c0:c1], start=True, stop=True)
+
+        quarter = keep.tile([P, 1], F32, name="quarter")
+        nc.vector.memset(quarter[:], 0.25)
+        warm = keep.tile([P, 1], F32, name="warm")
+        nc.scalar.activation(out=warm[:], in_=quarter[:], func=ACT.Abs_reciprocal_sqrt, bias=quarter[:])
+
+        xs_all = keep.tile([P, T], U8, name="xs_all")
+
+        offs_l = load_list("offs_l", offs)
+        two_l = load_list("two_l", two)
+        for q in range(4):
+            nc.sync.dma_start(out=xs_all[32 * q : 32 * q + 32, :].bitcast(I32),
+                              in_=x_scales[0, 4 * q : 4 * q + 4, :].bitcast(I32).partition_broadcast(8))
+        xw_all = keep.tile([P, T], I32, name="xw_all")
+        nc.sync.dma_start(out=xw_all[:], in_=x_words[0].rearrange("p c r -> p (c r)").bitcast(I32))
+        w1_raw = [load_weight_half("w1_raw%d" % a, w1, a) for a in range(2)]
+        w3_raw = [load_weight_half("w3_raw%d" % a, w3, a) for a in range(2)]
+        gain = keep.tile([P, PACK], F32, name="gain")
+        nc.sync.dma_start(out=gain[:], in_=gn.rearrange("(p t) o -> p (t o)", t=PACK))
+        n1_l = load_list("n1_l", n1)
+        n2_l = load_list("n2_l", n2)
+        w2_raw = [load_weight_half("w2_raw%d" % a, w2, a) for a in range(2)]
+        n4_l = load_list("n4_l", n4)
+        n3_l = load_list("n3_l", n3)
+
+        sq_win = [keep.tile([P, WINDOW], F32, name="sq_win%d" % t) for t in range(PACK)]
+        y_win = [keep.tile([P, WINDOW], F32, name="y_win%d" % t) for t in range(PACK)]
+        for t in range(PACK):
+            nc.vector.memset(sq_win[t][:, S:], 0.0)
+        ident = keep.tile([P, P], F32, name="ident")
+        make_identity(nc, ident[:])
+
+        def turn(dst, src, start, stop):
+            nc.tensor.matmul(dst, lhsT=src, rhs=ident[:], is_transpose=True, start=start, stop=stop)
+
+        def pick(name, dtype, table, lst):
+            got = keep.tile([P, S], dtype, name=name, align_bytes=64)
+            nc.vector.tensor_copy(got[:], table.indirect(lst[:]))
+            return got
+
+        def mx_tiles(name):
+            grouped = keep.tile([P, PACK * N], BF16, name=name + "_g", tag=name + "_g", align_bytes=64)
+            codes = keep.tile([P, N], U32, name=name + "_q", align_bytes=64)
+            scales = keep.tile([P, N], U8, name=name + "_s", align_bytes=64)
+            return grouped, codes, scales
+
+        xa_s = pick("xa_s", U8, xs_all[:], offs_l)
+        xb_s = pick("xb_s", U8, xs_all[:], two_l)
+        xa_w = pick("xa_w", U32, xw_all[:].bitcast(U32), offs_l)
+        xb_w = pick("xb_w", U32, xw_all[:].bitcast(U32), two_l)
+        w1_g, w1_q, w1_s = mx_tiles("w1")
+        nc.scalar.copy(*weave_views(w1_g, w1_raw[0], 0, 0, 64))
+        nc.scalar.copy(*weave_views(w1_g, w1_raw[1], 1, 0, 32))
+        nc.vector.tensor_copy(*weave_views(w1_g, w1_raw[1], 1, 32, 64))
+        y_bank = [psum.tile([P, S], F32, name="bank%d" % t, tag="bank%d" % t) for t in range(PACK)]
+        for t in range(PACK):
+            quantize(w1_q, w1_s, w1_g, t * P, (t + 1) * P)
+            product(y_bank[t], w1_q, w1_s, t, xa_w, xa_s, 0, S)
+
+        blocks = [slice(b * P, (b + 1) * P) for b in range(S // P)]
+        w3_g, w3_q, w3_s = mx_tiles("w3")
+        w2_g, w2_q, w2_s = mx_tiles("w2")
+        ssum = [keep.tile([P, S], F32, name="ssum%d" % t) for t in range(PACK)]
+        rinv = [keep.tile([P, S], F32, name="rinv%d" % t) for t in range(PACK)]
+        z = keep.tile([P, PACK, S], F32, name="z")
+
+        def sum_squares(t):
+            nc.scalar.activation(out=sq_win[t][:, :S], in_=y_bank[t][:], func=ACT.Square)
+            nc.scalar.activation(out=y_win[t][:, S:], in_=y_bank[t][:], func=ACT.Square)
+            nc.vector.tensor_tensor(ssum[t][:], sq_win[t][:].indirect(n1_l[:]), y_win[t][:, S:], ALU.add)
+
+        def make_z(t):
+            nc.scalar.activation(out=y_win[t][:, :S], in_=y_bank[t][:], func=ACT.Copy, scale=gain[:, t : t + 1])
+            nc.scalar.activation(out=rinv[t][:], in_=ssum[t][:], func=ACT.Abs_reciprocal_sqrt, bias=quarter[:])
+            nc.vector.tensor_tensor(z[:, t, :], y_win[t][:].indirect(n2_l[:]), rinv[t][:], ALU.mult)
+
+        for a in range(2):
+            dst, src = weave_views(w3_g, w3_raw[a], a, 0, 64)
+            nc.vector.tensor_scalar(dst, src, -1.0, None, ALU.mult)
+        quantize(w3_q, w3_s, w3_g, 0, N)
+        sum_squares(0)
+        for t in range(1, PACK):
+            sum_squares(t)
+            make_z(t - 1)
+        make_z(PACK - 1)
+        d_bank = [psum.tile([P, S], F32, name="dbank%d" % t, tag="side%d" % t) for t in range(PACK)]
+        for t in range(PACK):
+            product(d_bank[t], w3_q, w3_s, t, xb_w, xb_s, 0, S)
+
+        for a in range(2):
+            nc.scalar.copy(*weave_views(w2_g, w2_raw[a], a, 0, 64))
+        quantize(w2_q, w2_s, w2_g, 0, N)
+        z_g, z_q, z_s = mx_tiles("z")
+        for a, copy in enumerate((nc.vector.tensor_copy, nc.scalar.copy)):
+            c0, c1 = a * S // 2, (a + 1) * S // 2
+            copy(out=z_g[:, PACK * c0 : PACK * c1].rearrange("p (c i t) -> p c t i", i=4, t=PACK),
+                                  in_=z[:, :, c0:c1].rearrange("p t (c i) -> p c t i", i=4))
+        for a in range(2):
+            quantize(z_q, z_s, z_g, a * S // 2, (a + 1) * S // 2)
+        h_bank = [psum.tile([P, S], F32, name="hbank%d" % t, tag="bank%d" % t) for t in range(PACK)]
+        for t in range(PACK):
+            product(h_bank[t], w2_q, w2_s, t, z_q, z_s, 0, S)
+
+        d_win = y_win
+        d_got = [keep.tile([P, S], F32, name="d_got%d" % t) for t in range(PACK)]
+        for t in range(PACK):
+            nc.scalar.copy(out=d_win[t][:, :S], in_=d_bank[t][:])
+            nc.vector.tensor_copy(d_got[t][:], d_win[t][:].indirect(n4_l[:]))
+
+        out_rows = out.rearrange("(p t) c -> t p c", t=PACK)
+        for t in range(PACK):
+            h_win = sq_win[t]
+            nc.scalar.copy(out=h_win[:, :S], in_=h_bank[t][:])
+            high = keep.tile([P, S], F32, name="high%d" % t)
+            nc.vector.scalar_tensor_tensor(high[:], d_got[t][:], -1.0, h_bank[t][:], ALU.mult, ALU.max)
+            res = keep.tile([P, S], F32, name="res%d" % t)
+            if t == PACK - 1:
+                h_got = keep.tile([P, S], F32, name="h_got")
+                nc.vector.tensor_copy(h_got[:], h_win[:].indirect(n3_l[:]))
+                low = keep.tile([P, S], F32, name="low")
+                nc.vector.scalar_tensor_tensor(low[:], h_got[:], -1.0, d_bank[t][:], ALU.mult, ALU.max)
+                nc.vector.tensor_tensor(res[:], high[:], low[:], ALU.add)
+            else:
+                gap = keep.tile([P, S], F32, name="gap%d" % t)
+                nc.vector.tensor_tensor(gap[:], h_win[:].indirect(n3_l[:]), d_win[t][:, :S], ALU.add)
+                lift = keep.tile([P, S], F32, name="lift%d" % t)
+                nc.scalar.activation(out=lift[:], in_=gap[:], func=ACT.Relu, scale=-1.0)
+                sum_bank = psum.tile([P, S], F32, name="sumbank%d" % t, tag="side%d" % t)
+                terms = (d_win[t], high, lift)
+                for i, term in enumerate(terms):
+                    for b in range(PACK):
+                        turn(sum_bank[:, blocks[b]], term[:, blocks[b]], i == 0 and b == 0, i == len(terms) - 1 and b == PACK - 1)
+                res_t = keep.tile([P, S], F32, name="res_t%d" % t)
+                nc.scalar.copy(out=res_t[:], in_=sum_bank[:])
+                back_bank = psum.tile([P, S], F32, name="backbank%d" % t, tag="bank%d" % t)
+                for b in range(PACK):
+                    turn(back_bank[:, blocks[b]], res_t[:, blocks[b]], True, True)
+                nc.scalar.copy(out=res[:], in_=back_bank[:])
+            nc.sync.dma_start(out=out_rows[t], in_=res[:])

@@ -42,6 +42,10 @@ def tile_picked_latemaxbrms_none_p_kernel(tc, x_words, x_scales, w1, gn, w2, w3,
             dst = grouped[:].rearrange("p (t m j) -> p m j t", t=PACK, j=PACK)[:, half * P // 2 + m0 : half * P // 2 + m1]
             return dst, raw[:].rearrange("p j (m t) -> p m j t", t=PACK)[:, m0:m1]
 
+        def weave_views4(grouped, raw, half):
+            dst = grouped[:].rearrange("p (t g i j) -> p g t j i", t=PACK, i=4, j=PACK)[:, 16 * half : 16 * half + 16]
+            return dst, raw[:].rearrange("p j (g t i) -> p g t j i", t=PACK, i=4)
+
         def quantize(codes, scales, grouped, c0, c1):
             nc.vector.quantize_mx(out=codes[:, c0:c1].bitcast(FP8X4), scales=scales[:, c0:c1], in_=grouped[:, PACK * c0 : PACK * c1])
 
@@ -125,9 +129,8 @@ def tile_picked_latemaxbrms_none_p_kernel(tc, x_words, x_scales, w1, gn, w2, w3,
             nc.scalar.activation(out=rinv[t][:], in_=ssum[t][:], func=ACT.Abs_reciprocal_sqrt, bias=quarter[:])
             nc.vector.tensor_tensor(z[:, t, :], y_win[t][:].indirect(n2_l[:]), rinv[t][:], ALU.mult)
 
-        for a in range(2):
-            dst, src = weave_views(w3_g, w3_raw[a], a, 0, 64)
-            nc.vector.tensor_scalar(dst, src, -1.0, None, ALU.mult)
+        nc.scalar.copy(*weave_views4(w3_g, w3_raw[0], 0))
+        nc.vector.tensor_copy(*weave_views4(w3_g, w3_raw[1], 1))
         quantize(w3_q, w3_s, w3_g, 0, N)
         sum_squares(0)
         for t in range(1, PACK):
@@ -139,7 +142,7 @@ def tile_picked_latemaxbrms_none_p_kernel(tc, x_words, x_scales, w1, gn, w2, w3,
             product(d_bank[t], w3_q, w3_s, t, xb_w, xb_s, 0, S)
 
         for a in range(2):
-            nc.scalar.copy(*weave_views(w2_g, w2_raw[a], a, 0, 64))
+            nc.scalar.copy(*weave_views4(w2_g, w2_raw[a], a))
         quantize(w2_q, w2_s, w2_g, 0, N)
         z_g, z_q, z_s = mx_tiles("z")
         for a, copy in enumerate((nc.vector.tensor_copy, nc.scalar.copy)):
@@ -152,39 +155,69 @@ def tile_picked_latemaxbrms_none_p_kernel(tc, x_words, x_scales, w1, gn, w2, w3,
         for t in range(PACK):
             product(h_bank[t], w2_q, w2_s, t, z_q, z_s, 0, S)
 
-        d_win = y_win
-        d_got = [keep.tile([P, S], F32, name="d_got%d" % t) for t in range(PACK)]
-        for t in range(PACK):
-            nc.scalar.copy(out=d_win[t][:, :S], in_=d_bank[t][:])
-            nc.vector.tensor_copy(d_got[t][:], d_win[t][:].indirect(n4_l[:]))
+        d_win = [y_win[0], y_win[1], y_win[2], y_win[1]]
+        h_win = sq_win
+        out_rows = out.rearrange("(g t i) c -> t g i c", t=PACK, i=4)
 
-        out_rows = out.rearrange("(p t) c -> t p c", t=PACK)
-        for t in range(PACK):
-            h_win = sq_win[t]
-            nc.scalar.copy(out=h_win[:, :S], in_=h_bank[t][:])
+        def leave_d(t):
+            nc.scalar.activation(out=d_win[t][:, :S], in_=d_bank[t][:], func=ACT.Copy, scale=-1.0)
+
+        def fetch_d(t):
+            got = keep.tile([P, S], F32, name="d_got%d" % t)
+            nc.vector.tensor_copy(got[:], d_win[t][:].indirect(n4_l[:]))
+            return got
+
+        def larger(t, d_got):
             high = keep.tile([P, S], F32, name="high%d" % t)
-            nc.vector.scalar_tensor_tensor(high[:], d_got[t][:], -1.0, h_bank[t][:], ALU.mult, ALU.max)
-            res = keep.tile([P, S], F32, name="res%d" % t)
-            if t == PACK - 1:
-                h_got = keep.tile([P, S], F32, name="h_got")
-                nc.vector.tensor_copy(h_got[:], h_win[:].indirect(n3_l[:]))
-                low = keep.tile([P, S], F32, name="low")
-                nc.vector.scalar_tensor_tensor(low[:], h_got[:], -1.0, d_bank[t][:], ALU.mult, ALU.max)
-                nc.vector.tensor_tensor(res[:], high[:], low[:], ALU.add)
-            else:
-                gap = keep.tile([P, S], F32, name="gap%d" % t)
-                nc.vector.tensor_tensor(gap[:], h_win[:].indirect(n3_l[:]), d_win[t][:, :S], ALU.add)
-                lift = keep.tile([P, S], F32, name="lift%d" % t)
-                nc.scalar.activation(out=lift[:], in_=gap[:], func=ACT.Relu, scale=-1.0)
-                sum_bank = psum.tile([P, S], F32, name="sumbank%d" % t, tag="side%d" % t)
-                terms = (d_win[t], high, lift)
-                for i, term in enumerate(terms):
-                    for b in range(PACK):
-                        turn(sum_bank[:, blocks[b]], term[:, blocks[b]], i == 0 and b == 0, i == len(terms) - 1 and b == PACK - 1)
-                res_t = keep.tile([P, S], F32, name="res_t%d" % t)
-                nc.scalar.copy(out=res_t[:], in_=sum_bank[:])
-                back_bank = psum.tile([P, S], F32, name="backbank%d" % t, tag="bank%d" % t)
+            nc.vector.scalar_tensor_tensor(high[:], d_got[:], -1.0, h_bank[t][:], ALU.mult, ALU.max)
+            return high
+
+        def shortfall(name, win, lst, other):
+            gap = keep.tile([P, S], F32, name="gap" + name)
+            nc.vector.tensor_tensor(gap[:], win[:].indirect(lst[:]), other[:, :S], ALU.add)
+            lift = keep.tile([P, S], F32, name="lift" + name)
+            nc.scalar.activation(out=lift[:], in_=gap[:], func=ACT.Relu, scale=-1.0)
+            return lift
+
+        def add_and_store(t, terms):
+            sum_bank = psum.tile([P, S], F32, name="sumbank%d" % t, tag="side%d" % t)
+            for i, term in enumerate(terms):
                 for b in range(PACK):
-                    turn(back_bank[:, blocks[b]], res_t[:, blocks[b]], True, True)
-                nc.scalar.copy(out=res[:], in_=back_bank[:])
+                    turn(sum_bank[:, blocks[b]], term[:, blocks[b]], i == 0 and b == 0, i == len(terms) - 1 and b == PACK - 1)
+            res_t = keep.tile([P, S], F32, name="res_t%d" % t)
+            nc.scalar.copy(out=res_t[:], in_=sum_bank[:])
+            back_bank = psum.tile([P, S], F32, name="backbank%d" % t, tag="bank%d" % t)
+            for b in range(PACK):
+                turn(back_bank[:, blocks[b]], res_t[:, blocks[b]], True, True)
+            res = keep.tile([P, S], F32, name="res%d" % t)
+            nc.scalar.copy(out=res[:], in_=back_bank[:])
             nc.sync.dma_start(out=out_rows[t], in_=res[:])
+
+        d_got = []
+        for t in range(2):
+            leave_d(t)
+            d_got.append(fetch_d(t))
+        leave_d(2)
+        for t in range(3):
+            nc.scalar.copy(out=h_win[t][:, :S], in_=h_bank[t][:])
+        for t in range(2):
+            high = larger(t, d_got[t])
+            add_and_store(t, (d_win[t], high, shortfall("h%d" % t, h_win[t], n3_l, d_win[t])))
+        lift_d = shortfall("d2", d_win[2], n4_l, h_win[2])
+        lift_h = shortfall("h2", h_win[2], n3_l, d_win[2])
+        leave_d(3)
+        nc.scalar.copy(out=h_win[3][:, :S], in_=h_bank[3][:])
+        add_and_store(2, (d_win[2], h_win[2], lift_d, lift_h))
+
+        t = PACK - 1
+        high = larger(t, fetch_d(t))
+        h_got = keep.tile([P, S], F32, name="h_got")
+        nc.vector.tensor_copy(h_got[:], h_win[t][:].indirect(n3_l[:]))
+        halves = [slice(0, S // 2), slice(S // 2, S)]
+        low = [keep.tile([P, S // 2], F32, name="low%d" % a) for a in range(2)]
+        for a in range(2):
+            nc.vector.tensor_tensor(low[a][:], h_got[:, halves[a]], d_bank[t][:, halves[a]], ALU.min)
+        for a in range(2):
+            res = keep.tile([P, S // 2], F32, name="last%d" % a)
+            nc.vector.tensor_tensor(res[:], high[:, halves[a]], low[a][:], ALU.subtract)
+            nc.sync.dma_start(out=out_rows[t][:, :, halves[a]], in_=res[:])

@@ -19,6 +19,7 @@ ACT = mybir.ActivationFunctionType
 P = 128
 PACK = 4
 WINDOW = 2 * S
+EARLY = 2
 
 
 def tile_picked_latemaxbrms_none_p_kernel(tc, x_words, x_scales, w1, gn, w2, w3, offs, n1, n2, two, n3, n4, out):
@@ -49,10 +50,10 @@ def tile_picked_latemaxbrms_none_p_kernel(tc, x_words, x_scales, w1, gn, w2, w3,
         def quantize(codes, scales, grouped, c0, c1):
             nc.vector.quantize_mx(out=codes[:, c0:c1].bitcast(FP8X4), scales=scales[:, c0:c1], in_=grouped[:, PACK * c0 : PACK * c1])
 
-        def product(bank, wq, ws, t, xq, xs, c0, c1):
+        def product(bank, wq, ws, t, xq, xs, c0, c1, start=True, stop=True):
             cols = slice(t * P, (t + 1) * P)
             nc.tensor.matmul_mx(out=bank[:, c0:c1], lhsT=wq[:, cols].bitcast(FP8X4), lhsT_scale=ws[:, cols],
-                                rhs=xq[:, c0:c1].bitcast(FP8X4), rhs_scale=xs[:, c0:c1], start=True, stop=True)
+                                rhs=xq[:, c0:c1].bitcast(FP8X4), rhs_scale=xs[:, c0:c1], start=start, stop=stop)
 
         quarter = keep.tile([P, 1], F32, name="quarter")
         nc.vector.memset(quarter[:], 0.25)
@@ -72,6 +73,8 @@ def tile_picked_latemaxbrms_none_p_kernel(tc, x_words, x_scales, w1, gn, w2, w3,
         w3_raw = [load_weight_half("w3_raw%d" % a, w3, a) for a in range(2)]
         gain = keep.tile([P, PACK], F32, name="gain")
         nc.sync.dma_start(out=gain[:], in_=gn.rearrange("(p t) o -> p (t o)", t=PACK))
+        gain_neg = keep.tile([P, PACK], F32, name="gain_neg")
+        nc.vector.tensor_scalar(gain_neg[:], gain[:], -1.0, None, ALU.mult)
         n1_l = load_list("n1_l", n1)
         n2_l = load_list("n2_l", n2)
         w2_raw = [load_weight_half("w2_raw%d" % a, w2, a) for a in range(2)]
@@ -125,7 +128,7 @@ def tile_picked_latemaxbrms_none_p_kernel(tc, x_words, x_scales, w1, gn, w2, w3,
             nc.vector.tensor_tensor(ssum[t][:], sq_win[t][:].indirect(n1_l[:]), y_win[t][:, S:], ALU.add)
 
         def make_z(t):
-            nc.scalar.activation(out=y_win[t][:, :S], in_=y_bank[t][:], func=ACT.Copy, scale=gain[:, t : t + 1])
+            nc.scalar.activation(out=y_win[t][:, :S], in_=y_bank[t][:], func=ACT.Copy, scale=gain_neg[:, t : t + 1])
             nc.scalar.activation(out=rinv[t][:], in_=ssum[t][:], func=ACT.Abs_reciprocal_sqrt, bias=quarter[:])
             nc.vector.tensor_tensor(z[:, t, :], y_win[t][:].indirect(n2_l[:]), rinv[t][:], ALU.mult)
 
@@ -141,35 +144,38 @@ def tile_picked_latemaxbrms_none_p_kernel(tc, x_words, x_scales, w1, gn, w2, w3,
         for t in range(PACK):
             product(d_bank[t], w3_q, w3_s, t, xb_w, xb_s, 0, S)
 
-        for a in range(2):
-            nc.scalar.copy(*weave_views4(w2_g, w2_raw[a], a))
-        quantize(w2_q, w2_s, w2_g, 0, N)
-        z_g, z_q, z_s = mx_tiles("z")
-        for a, copy in enumerate((nc.vector.tensor_copy, nc.scalar.copy)):
-            c0, c1 = a * S // 2, (a + 1) * S // 2
-            copy(out=z_g[:, PACK * c0 : PACK * c1].rearrange("p (c i t) -> p c t i", i=4, t=PACK),
-                                  in_=z[:, :, c0:c1].rearrange("p t (c i) -> p c t i", i=4))
-        for a in range(2):
-            quantize(z_q, z_s, z_g, a * S // 2, (a + 1) * S // 2)
-        h_bank = [psum.tile([P, S], F32, name="hbank%d" % t, tag="bank%d" % t) for t in range(PACK)]
-        for t in range(PACK):
-            product(h_bank[t], w2_q, w2_s, t, z_q, z_s, 0, S)
-
-        d_win = [y_win[0], y_win[1], y_win[2], y_win[1]]
+        d_win = y_win
         h_win = sq_win
         out_rows = out.rearrange("(g t i) c -> t g i c", t=PACK, i=4)
 
         def leave_d(t):
-            nc.scalar.activation(out=d_win[t][:, :S], in_=d_bank[t][:], func=ACT.Copy, scale=-1.0)
+            nc.scalar.activation(out=d_win[t][:, :S], in_=d_bank[t][:], func=ACT.Copy, scale=-1.0 if t < EARLY else 1.0)
 
         def fetch_d(t):
             got = keep.tile([P, S], F32, name="d_got%d" % t)
             nc.vector.tensor_copy(got[:], d_win[t][:].indirect(n4_l[:]))
             return got
 
+        z_g, z_q, z_s = mx_tiles("z")
+        for a in range(2):
+            nc.scalar.copy(*weave_views4(w2_g, w2_raw[a], a))
+        quantize(w2_q, w2_s, w2_g, 0, N)
+        nc.vector.tensor_copy(out=z_g[:, PACK * 0 : PACK * 256].rearrange("p (c i t) -> p c t i", i=4, t=PACK), in_=z[:, :, 0:256].rearrange("p t (c i) -> p c t i", i=4))
+        nc.scalar.copy(out=z_g[:, PACK * 256 : PACK * 512].rearrange("p (c i t) -> p c t i", i=4, t=PACK), in_=z[:, :, 256:512].rearrange("p t (c i) -> p c t i", i=4))
+        quantize(z_q, z_s, z_g, 0, 256)
+        quantize(z_q, z_s, z_g, 256, 512)
+        d_got = []
+        for t in range(2):
+            leave_d(t)
+            d_got.append(fetch_d(t))
+        leave_d(2)
+        h_bank = [psum.tile([P, S], F32, name="hbank%d" % t, tag="bank%d" % t) for t in range(PACK)]
+        for t in range(PACK):
+            product(h_bank[t], w2_q, w2_s, t, z_q, z_s, 0, S)
+
         def larger(t, d_got):
             high = keep.tile([P, S], F32, name="high%d" % t)
-            nc.vector.scalar_tensor_tensor(high[:], d_got[:], -1.0, h_bank[t][:], ALU.mult, ALU.max)
+            nc.vector.scalar_tensor_tensor(high[:], d_got[:], -1.0, h_win[t][:, :S], ALU.mult, ALU.max)
             return high
 
         def shortfall(name, win, lst, other):
@@ -193,31 +199,68 @@ def tile_picked_latemaxbrms_none_p_kernel(tc, x_words, x_scales, w1, gn, w2, w3,
             nc.scalar.copy(out=res[:], in_=back_bank[:])
             nc.sync.dma_start(out=out_rows[t], in_=res[:])
 
-        d_got = []
-        for t in range(2):
-            leave_d(t)
-            d_got.append(fetch_d(t))
-        leave_d(2)
-        for t in range(3):
-            nc.scalar.copy(out=h_win[t][:, :S], in_=h_bank[t][:])
-        for t in range(2):
-            high = larger(t, d_got[t])
-            add_and_store(t, (d_win[t], high, shortfall("h%d" % t, h_win[t], n3_l, d_win[t])))
-        lift_d = shortfall("d2", d_win[2], n4_l, h_win[2])
-        lift_h = shortfall("h2", h_win[2], n3_l, d_win[2])
-        leave_d(3)
-        nc.scalar.copy(out=h_win[3][:, :S], in_=h_bank[3][:])
-        add_and_store(2, (d_win[2], h_win[2], lift_d, lift_h))
+        def leave(win, bank, sign):
+            nc.scalar.activation(out=win[:, :S], in_=bank[:], func=ACT.Copy, scale=sign)
 
-        t = PACK - 1
-        high = larger(t, fetch_d(t))
-        h_got = keep.tile([P, S], F32, name="h_got")
-        nc.vector.tensor_copy(h_got[:], h_win[t][:].indirect(n3_l[:]))
-        halves = [slice(0, S // 2), slice(S // 2, S)]
-        low = [keep.tile([P, S // 2], F32, name="low%d" % a) for a in range(2)]
-        for a in range(2):
-            nc.vector.tensor_tensor(low[a][:], h_got[:, halves[a]], d_bank[t][:, halves[a]], ALU.min)
-        for a in range(2):
-            res = keep.tile([P, S // 2], F32, name="last%d" % a)
-            nc.vector.tensor_tensor(res[:], high[:, halves[a]], low[a][:], ALU.subtract)
-            nc.sync.dma_start(out=out_rows[t][:, :, halves[a]], in_=res[:])
+        def add_turned(name, tag, terms):
+            bank = psum.tile([P, S], F32, name=name, tag=tag)
+            for i, term in enumerate(terms):
+                for b in range(PACK):
+                    turn(bank[:, blocks[b]], term[:, blocks[b]], i == 0 and b == 0, i == len(terms) - 1 and b == PACK - 1)
+            return bank
+
+        def fetch_add(name, win, lst, other):
+            got = keep.tile([P, S], F32, name=name)
+            nc.vector.tensor_tensor(got[:], win[:].indirect(lst[:]), other[:, :S], ALU.add)
+            return got
+
+        def late_base(t):
+            bank = add_turned("e_bank%d" % t, "side%d" % t, (d_win[t], h_win[t]))
+            e_t = keep.tile([P, S], F32, name="e_t%d" % t)
+            leave(e_t, bank, 1.0)
+            return e_t
+
+        def late_high(t, e_t):
+            over = fetch_add("over%d" % t, d_win[t], n4_l, h_win[t])
+            bank = add_turned("o_bank%d" % t, "bank%d" % t, (over,))
+            r_t = keep.tile([P, S], F32, name="r_t%d" % t)
+            nc.scalar.activation(out=r_t[:], in_=bank[:], func=ACT.Relu)
+            return add_turned("m_bank%d" % t, "side%d" % t, (e_t, r_t))
+
+        def late_finish(t, m_bank, parts):
+            under = fetch_add("under%d" % t, h_win[t], n3_l, d_win[t])
+            for a in range(parts):
+                cols = slice(a * S // parts, (a + 1) * S // parts)
+                res = keep.tile([P, S // parts], F32, name="res%d_%d" % (t, a))
+                nc.vector.scalar_tensor_tensor(res[:], under[:, cols], 0.0, m_bank[:, cols], ALU.max, ALU.add)
+                nc.sync.dma_start(out=out_rows[t][:, :, cols], in_=res[:])
+
+        def base_back(t):
+            return add_turned("m_bank%d" % t, "bank%d" % t, (late_base(t),))
+
+        def two_step(t, e_bank, parts):
+            over = fetch_add("over%d" % t, d_win[t], n4_l, h_win[t])
+            under = fetch_add("under%d" % t, h_win[t], n3_l, d_win[t])
+            high = keep.tile([P, S], F32, name="high%d" % t)
+            for a in range(parts):
+                cols = slice(a * S // parts, (a + 1) * S // parts)
+                nc.vector.scalar_tensor_tensor(high[:, cols], over[:, cols], 0.0, e_bank[:, cols], ALU.max, ALU.subtract)
+            for a in range(parts):
+                cols = slice(a * S // parts, (a + 1) * S // parts)
+                res = keep.tile([P, S // parts], F32, name="res%d_%d" % (t, a))
+                nc.vector.scalar_tensor_tensor(res[:], under[:, cols], 0.0, high[:, cols], ALU.max, ALU.add)
+                nc.sync.dma_start(out=out_rows[t][:, :, cols], in_=res[:])
+
+        for t in range(PACK):
+            leave(h_win[t], h_bank[t], -1.0 if t < EARLY else 1.0)
+        leave_d(3)
+        lift0 = shortfall("h0", h_win[0], n3_l, d_win[0])
+        add_and_store(0, (d_win[0], larger(0, d_got[0]), lift0))
+        lift1 = shortfall("h1", h_win[1], n3_l, d_win[1])
+        add_and_store(1, (d_win[1], larger(1, d_got[1]), lift1))
+        e2 = base_back(2)
+        e3 = psum.tile([P, S], F32, name="e3", tag="side3")
+        product(e3, w3_q, w3_s, 3, xb_w, xb_s, 0, S, stop=False)
+        product(e3, w2_q, w2_s, 3, z_q, z_s, 0, S, start=False)
+        two_step(2, e2, 1)
+        two_step(3, e3, 2)

@@ -55,18 +55,20 @@ def tile_picked_latemaxbrms_none_p_kernel(tc, x_words, x_scales, w1, gn, w2, w3,
             nc.tensor.matmul_mx(out=bank[:, c0:c1], lhsT=wq[:, cols].bitcast(FP8X4), lhsT_scale=ws[:, cols],
                                 rhs=xq[:, c0:c1].bitcast(FP8X4), rhs_scale=xs[:, c0:c1], start=start, stop=stop)
 
+        xs_all = keep.tile([P, T], U8, name="xs_all")
+        nc.vector.memset(xs_all[:, : T // 2].bitcast(I32), 0)
+        nc.gpsimd.memset(xs_all[:, T // 2 :].bitcast(I32), 0)
         quarter = keep.tile([P, 1], F32, name="quarter")
         nc.vector.memset(quarter[:], 0.25)
         warm = keep.tile([P, 1], F32, name="warm")
         nc.scalar.activation(out=warm[:], in_=quarter[:], func=ACT.Abs_reciprocal_sqrt, bias=quarter[:])
 
-        xs_all = keep.tile([P, T], U8, name="xs_all")
 
         offs_l = load_list("offs_l", offs)
         two_l = load_list("two_l", two)
+        n1_l = load_list("n1_l", n1)
         for q in range(4):
-            nc.sync.dma_start(out=xs_all[32 * q : 32 * q + 32, :].bitcast(I32),
-                              in_=x_scales[0, 4 * q : 4 * q + 4, :].bitcast(I32).partition_broadcast(8))
+            nc.sync.dma_start(out=xs_all[32 * q : 32 * q + 4, :].bitcast(I32), in_=x_scales[0, 4 * q : 4 * q + 4, :].bitcast(I32))
         xw_all = keep.tile([P, T], I32, name="xw_all")
         nc.sync.dma_start(out=xw_all[:], in_=x_words[0].rearrange("p c r -> p (c r)").bitcast(I32))
         w1_raw = [load_weight_half("w1_raw%d" % a, w1, a) for a in range(2)]
@@ -75,7 +77,6 @@ def tile_picked_latemaxbrms_none_p_kernel(tc, x_words, x_scales, w1, gn, w2, w3,
         nc.sync.dma_start(out=gain[:], in_=gn.rearrange("(p t) o -> p (t o)", t=PACK))
         gain_neg = keep.tile([P, PACK], F32, name="gain_neg")
         nc.vector.tensor_scalar(gain_neg[:], gain[:], -1.0, None, ALU.mult)
-        n1_l = load_list("n1_l", n1)
         n2_l = load_list("n2_l", n2)
         w2_raw = [load_weight_half("w2_raw%d" % a, w2, a) for a in range(2)]
         n4_l = load_list("n4_l", n4)

from contextlib import ExitStack

import concourse.mybir as mybir
from concourse.masks import make_identity

K, T, S, N, H = 512, 2048, 512, 512, 512
FLOPS = 3 * 2 * 512 * 512 * 512

F32 = mybir.dt.float32
BF16 = mybir.dt.bfloat16
I32 = mybir.dt.int32
U32 = mybir.dt.uint32
U16 = mybir.dt.uint16
U8 = mybir.dt.uint8
FP8X4 = mybir.dt.float8_e4m3fn_x4
ALU = mybir.AluOpType
ACT = mybir.ActivationFunctionType

P = 128
PACK = 4
WINDOW = 2 * S
EARLY = 2


def tile_picked_latemaxbrms_none_p_kernel(tc, x_words, x_scales, w1, gn, w2, w3, offs, n1, n2, two, n3, n4, out):
    nc = tc.nc
    with ExitStack() as ctx:
        keep = ctx.enter_context(tc.tile_pool(name="keep", bufs=1))
        psum = ctx.enter_context(tc.psum_pool(name="psum", bufs=1))

        def load_list(name, src):
            lst = keep.tile([P, S // 16], U16, name=name)
            nc.sync.dma_start(lst[:], src)
            return lst

        def load_weight_half(name, w, half):
            raw = keep.tile([P, PACK, N // 2], F32, name=name)
            cols = slice(half * N // 2, (half + 1) * N // 2)
            nc.sync.dma_start(out=raw[:], in_=w[:, cols].rearrange("(p j) c -> p j c", j=PACK))
            return raw

        def weave_views(grouped, raw, half, m0, m1):
            dst = grouped[:].rearrange("p (t m j) -> p m j t", t=PACK, j=PACK)[:, half * P // 2 + m0 : half * P // 2 + m1]
            return dst, raw[:].rearrange("p j (m t) -> p m j t", t=PACK)[:, m0:m1]

        def weave_views4(grouped, raw, half):
            dst = grouped[:].rearrange("p (t g i j) -> p g t j i", t=PACK, i=4, j=PACK)[:, 16 * half : 16 * half + 16]
            return dst, raw[:].rearrange("p j (g t i) -> p g t j i", t=PACK, i=4)

        def quantize(codes, scales, grouped, c0, c1):
            nc.vector.quantize_mx(out=codes[:, c0:c1].bitcast(FP8X4), scales=scales[:, c0:c1], in_=grouped[:, PACK * c0 : PACK * c1])

        def product(bank, wq, ws, t, xq, xs, c0, c1, start=True, stop=True):
            cols = slice(t * P, (t + 1) * P)
            nc.tensor.matmul_mx(out=bank[:, c0:c1], lhsT=wq[:, cols].bitcast(FP8X4), lhsT_scale=ws[:, cols],
                                rhs=xq[:, c0:c1].bitcast(FP8X4), rhs_scale=xs[:, c0:c1], start=start, stop=stop)

        xs_all = keep.tile([P, T], U8, name="xs_all")
        nc.vector.memset(xs_all[:, : T // 2].bitcast(I32), 0)
        nc.gpsimd.memset(xs_all[:, T // 2 :].bitcast(I32), 0)
        quarter = keep.tile([P, 1], F32, name="quarter")
        nc.vector.memset(quarter[:], 0.25)
        warm = keep.tile([P, 1], F32, name="warm")
        nc.scalar.activation(out=warm[:], in_=quarter[:], func=ACT.Abs_reciprocal_sqrt, bias=quarter[:])


        offs_l = load_list("offs_l", offs)
        two_l = load_list("two_l", two)
        n1_l = load_list("n1_l", n1)
        for q in range(4):
            nc.sync.dma_start(out=xs_all[32 * q : 32 * q + 4, :].bitcast(I32), in_=x_scales[0, 4 * q : 4 * q + 4, :].bitcast(I32))
        xw_all = keep.tile([P, T], I32, name="xw_all")
        nc.sync.dma_start(out=xw_all[:], in_=x_words[0].rearrange("p c r -> p (c r)").bitcast(I32))
        w1_raw = [load_weight_half("w1_raw%d" % a, w1, a) for a in range(2)]
        w3_raw = [load_weight_half("w3_raw%d" % a, w3, a) for a in range(2)]
        gain = keep.tile([P, PACK], F32, name="gain")
        nc.sync.dma_start(out=gain[:], in_=gn.rearrange("(p t) o -> p (t o)", t=PACK))
        gain_neg = keep.tile([P, PACK], F32, name="gain_neg")
        nc.vector.tensor_scalar(gain_neg[:], gain[:], -1.0, None, ALU.mult)
        n2_l = load_list("n2_l", n2)
        w2_raw = [load_weight_half("w2_raw%d" % a, w2, a) for a in range(2)]
        n4_l = load_list("n4_l", n4)
        n3_l = load_list("n3_l", n3)

        sq_win = [keep.tile([P, WINDOW], F32, name="sq_win%d" % t) for t in range(PACK)]
        y_win = [keep.tile([P, WINDOW], F32, name="y_win%d" % t) for t in range(PACK)]
        for t in range(PACK):
            nc.vector.memset(sq_win[t][:, S:], 0.0)
        ident = keep.tile([P, P], F32, name="ident")
        make_identity(nc, ident[:])

        def turn(dst, src, start, stop):
            nc.tensor.matmul(dst, lhsT=src, rhs=ident[:], is_transpose=True, start=start, stop=stop)

        def pick(name, dtype, table, lst):
            got = keep.tile([P, S], dtype, name=name, align_bytes=64)
            nc.vector.tensor_copy(got[:], table.indirect(lst[:]))
            return got

        def mx_tiles(name):
            grouped = keep.tile([P, PACK * N], BF16, name=name + "_g", tag=name + "_g", align_bytes=64)
            codes = keep.tile([P, N], U32, name=name + "_q", align_bytes=64)
            scales = keep.tile([P, N], U8, name=name + "_s", align_bytes=64)
            return grouped, codes, scales

        xa_s = pick("xa_s", U8, xs_all[:], offs_l)
        xb_s = pick("xb_s", U8, xs_all[:], two_l)
        xa_w = pick("xa_w", U32, xw_all[:].bitcast(U32), offs_l)
        xb_w = pick("xb_w", U32, xw_all[:].bitcast(U32), two_l)
        w1_g, w1_q, w1_s = mx_tiles("w1")
        nc.scalar.copy(*weave_views(w1_g, w1_raw[0], 0, 0, 64))
        nc.scalar.copy(*weave_views(w1_g, w1_raw[1], 1, 0, 32))
        nc.vector.tensor_copy(*weave_views(w1_g, w1_raw[1], 1, 32, 64))
        y_bank = [psum.tile([P, S], F32, name="bank%d" % t, tag="bank%d" % t) for t in range(PACK)]
        for t in range(PACK):
            quantize(w1_q, w1_s, w1_g, t * P, (t + 1) * P)
            product(y_bank[t], w1_q, w1_s, t, xa_w, xa_s, 0, S)

        blocks = [slice(b * P, (b + 1) * P) for b in range(S // P)]
        w3_g, w3_q, w3_s = mx_tiles("w3")
        w2_g, w2_q, w2_s = mx_tiles("w2")
        ssum = [keep.tile([P, S], F32, name="ssum%d" % t) for t in range(PACK)]
        rinv = [keep.tile([P, S], F32, name="rinv%d" % t) for t in range(PACK)]
        z = keep.tile([P, PACK, S], F32, name="z")

        def sum_squares(t):
            nc.scalar.activation(out=sq_win[t][:, :S], in_=y_bank[t][:], func=ACT.Square)
            nc.scalar.activation(out=y_win[t][:, S:], in_=y_bank[t][:], func=ACT.Square)
            nc.vector.tensor_tensor(ssum[t][:], sq_win[t][:].indirect(n1_l[:]), y_win[t][:, S:], ALU.add)

        def make_z(t):
            nc.scalar.activation(out=y_win[t][:, :S], in_=y_bank[t][:], func=ACT.Copy, scale=gain_neg[:, t : t + 1])
            nc.scalar.activation(out=rinv[t][:], in_=ssum[t][:], func=ACT.Abs_reciprocal_sqrt, bias=quarter[:])
            nc.vector.tensor_tensor(z[:, t, :], y_win[t][:].indirect(n2_l[:]), rinv[t][:], ALU.mult)

        nc.scalar.copy(*weave_views4(w3_g, w3_raw[0], 0))
        nc.vector.tensor_copy(*weave_views4(w3_g, w3_raw[1], 1))
        quantize(w3_q, w3_s, w3_g, 0, N)
        sum_squares(0)
        for t in range(1, PACK):
            sum_squares(t)
            make_z(t - 1)
        make_z(PACK - 1)
        d_bank = [psum.tile([P, S], F32, name="dbank%d" % t, tag="side%d" % t) for t in range(PACK)]
        for t in range(PACK):
            product(d_bank[t], w3_q, w3_s, t, xb_w, xb_s, 0, S)

        d_win = y_win
        h_win = sq_win
        out_rows = out.rearrange("(g t i) c -> t g i c", t=PACK, i=4)

        def leave_d(t):
            nc.scalar.activation(out=d_win[t][:, :S], in_=d_bank[t][:], func=ACT.Copy, scale=-1.0 if t < EARLY else 1.0)

        def fetch_d(t):
            got = keep.tile([P, S], F32, name="d_got%d" % t)
            nc.vector.tensor_copy(got[:], d_win[t][:].indirect(n4_l[:]))
            return got

        z_g, z_q, z_s = mx_tiles("z")
        for a in range(2):
            nc.scalar.copy(*weave_views4(w2_g, w2_raw[a], a))
        quantize(w2_q, w2_s, w2_g, 0, N)
        nc.vector.tensor_copy(out=z_g[:, PACK * 0 : PACK * 256].rearrange("p (c i t) -> p c t i", i=4, t=PACK), in_=z[:, :, 0:256].rearrange("p t (c i) -> p c t i", i=4))
        nc.scalar.copy(out=z_g[:, PACK * 256 : PACK * 512].rearrange("p (c i t) -> p c t i", i=4, t=PACK), in_=z[:, :, 256:512].rearrange("p t (c i) -> p c t i", i=4))
        quantize(z_q, z_s, z_g, 0, 256)
        quantize(z_q, z_s, z_g, 256, 512)
        d_got = []
        for t in range(2):
            leave_d(t)
            d_got.append(fetch_d(t))
        leave_d(2)
        h_bank = [psum.tile([P, S], F32, name="hbank%d" % t, tag="bank%d" % t) for t in range(PACK)]
        for t in range(PACK):
            product(h_bank[t], w2_q, w2_s, t, z_q, z_s, 0, S)

        def larger(t, d_got):
            high = keep.tile([P, S], F32, name="high%d" % t)
            nc.vector.scalar_tensor_tensor(high[:], d_got[:], -1.0, h_win[t][:, :S], ALU.mult, ALU.max)
            return high

        def shortfall(name, win, lst, other):
            gap = keep.tile([P, S], F32, name="gap" + name)
            nc.vector.tensor_tensor(gap[:], win[:].indirect(lst[:]), other[:, :S], ALU.add)
            lift = keep.tile([P, S], F32, name="lift" + name)
            nc.scalar.activation(out=lift[:], in_=gap[:], func=ACT.Relu, scale=-1.0)
            return lift

        def add_and_store(t, terms):
            sum_bank = psum.tile([P, S], F32, name="sumbank%d" % t, tag="side%d" % t)
            for i, term in enumerate(terms):
                for b in range(PACK):
                    turn(sum_bank[:, blocks[b]], term[:, blocks[b]], i == 0 and b == 0, i == len(terms) - 1 and b == PACK - 1)
            res_t = keep.tile([P, S], F32, name="res_t%d" % t)
            nc.scalar.copy(out=res_t[:], in_=sum_bank[:])
            back_bank = psum.tile([P, S], F32, name="backbank%d" % t, tag="bank%d" % t)
            for b in range(PACK):
                turn(back_bank[:, blocks[b]], res_t[:, blocks[b]], True, True)
            res = keep.tile([P, S], F32, name="res%d" % t)
            nc.scalar.copy(out=res[:], in_=back_bank[:])
            nc.sync.dma_start(out=out_rows[t], in_=res[:])

        def leave(win, bank, sign):
            nc.scalar.activation(out=win[:, :S], in_=bank[:], func=ACT.Copy, scale=sign)

        def add_turned(name, tag, terms):
            bank = psum.tile([P, S], F32, name=name, tag=tag)
            for i, term in enumerate(terms):
                for b in range(PACK):
                    turn(bank[:, blocks[b]], term[:, blocks[b]], i == 0 and b == 0, i == len(terms) - 1 and b == PACK - 1)
            return bank

        def fetch_add(name, win, lst, other):
            got = keep.tile([P, S], F32, name=name)
            nc.vector.tensor_tensor(got[:], win[:].indirect(lst[:]), other[:, :S], ALU.add)
            return got

        def late_base(t):
            bank = add_turned("e_bank%d" % t, "side%d" % t, (d_win[t], h_win[t]))
            e_t = keep.tile([P, S], F32, name="e_t%d" % t)
            leave(e_t, bank, 1.0)
            return e_t

        def late_high(t, e_t):
            over = fetch_add("over%d" % t, d_win[t], n4_l, h_win[t])
            bank = add_turned("o_bank%d" % t, "bank%d" % t, (over,))
            r_t = keep.tile([P, S], F32, name="r_t%d" % t)
            nc.scalar.activation(out=r_t[:], in_=bank[:], func=ACT.Relu)
            return add_turned("m_bank%d" % t, "side%d" % t, (e_t, r_t))

        def late_finish(t, m_bank, parts):
            under = fetch_add("under%d" % t, h_win[t], n3_l, d_win[t])
            for a in range(parts):
                cols = slice(a * S // parts, (a + 1) * S // parts)
                res = keep.tile([P, S // parts], F32, name="res%d_%d" % (t, a))
                nc.vector.scalar_tensor_tensor(res[:], under[:, cols], 0.0, m_bank[:, cols], ALU.max, ALU.add)
                nc.sync.dma_start(out=out_rows[t][:, :, cols], in_=res[:])

        def base_back(t):
            return add_turned("m_bank%d" % t, "bank%d" % t, (late_base(t),))

        def two_step(t, e_bank, parts):
            over = fetch_add("over%d" % t, d_win[t], n4_l, h_win[t])
            under = fetch_add("under%d" % t, h_win[t], n3_l, d_win[t])
            high = keep.tile([P, S], F32, name="high%d" % t)
            for a in range(parts):
                cols = slice(a * S // parts, (a + 1) * S // parts)
                nc.vector.scalar_tensor_tensor(high[:, cols], over[:, cols], 0.0, e_bank[:, cols], ALU.max, ALU.subtract)
            for a in range(parts):
                cols = slice(a * S // parts, (a + 1) * S // parts)
                res = keep.tile([P, S // parts], F32, name="res%d_%d" % (t, a))
                nc.vector.scalar_tensor_tensor(res[:], under[:, cols], 0.0, high[:, cols], ALU.max, ALU.add)
                nc.sync.dma_start(out=out_rows[t][:, :, cols], in_=res[:])

        for t in range(PACK):
            leave(h_win[t], h_bank[t], -1.0 if t < EARLY else 1.0)
        leave_d(3)
        lift0 = shortfall("h0", h_win[0], n3_l, d_win[0])
        add_and_store(0, (d_win[0], larger(0, d_got[0]), lift0))
        lift1 = shortfall("h1", h_win[1], n3_l, d_win[1])
        add_and_store(1, (d_win[1], larger(1, d_got[1]), lift1))
        e2 = base_back(2)
        e3 = psum.tile([P, S], F32, name="e3", tag="side3")
        product(e3, w3_q, w3_s, 3, xb_w, xb_s, 0, S, stop=False)
        product(e3, w2_q, w2_s, 3, z_q, z_s, 0, S, start=False)
        two_step(2, e2, 1)
        two_step(3, e3, 2)
